import numpy as np
import ml_dtypes


def mxq(x, axis, fmt="e4m3"):
    dtype, down = {"e4m3": (ml_dtypes.float8_e4m3fn, 7), "e5m2": (ml_dtypes.float8_e5m2, 14)}[fmt]
    v = np.moveaxis(np.asarray(x, np.float32).astype(ml_dtypes.bfloat16).astype(np.float64), axis, -1)
    blocks = v.reshape(v.shape[:-1] + (-1, 32))
    amax = np.abs(blocks).max(-1, keepdims=True)
    byte = np.maximum(np.where(amax > 0, np.frexp(amax)[1] - 1 + 127, 0) - down, 1)
    scale = np.exp2(byte - 127.0)
    codes = (blocks / scale).astype(np.float32).astype(dtype).astype(np.float64)
    return np.moveaxis((codes * scale).reshape(v.shape), -1, axis)


WIDE = False


def mx_kscale(k):
    if not WIDE:
        return np.ones(k)
    levels = np.array([10, -10, 5, -5, 0])
    if k % 512:
        return np.exp2(np.random.permutation(np.resize(levels, k // 32))).repeat(32)
    a = np.empty((k // 512, 16))
    for p in range(k // 512):
        a[p, :8] = np.random.permutation(np.resize(levels, 8))
        for g in range(8):
            far = levels[np.abs(levels - a[p, g]) >= 10]
            a[p, g + 8] = far[np.random.randint(len(far))]
    return np.exp2(a.ravel()).repeat(32)


def f64(x):
    return np.asarray(x).astype(np.float64)


def striped(idx):
    return np.tile(np.asarray(idx).reshape(-1, 16).T, (8, 1)).astype(np.uint16)


def unstriped(offs):
    return offs[:16].T.reshape(-1).astype(np.int64)


E2M1 = np.array([0.0, 0.5, 1.0, 1.5, 2.0, 3.0, 4.0, 6.0, -0.0, -0.5, -1.0, -1.5, -2.0, -3.0, -4.0, -6.0])


def pack_weight(w, fmt):
    k, n = w.shape
    w = f64(np.asarray(w, np.float32).astype(ml_dtypes.bfloat16)).reshape(k // 32, 32, n)
    amax = np.abs(w).max(1)
    if fmt == "e4m3":
        byte = np.frexp(amax)[1] - 1 + 127 - 7
    else:
        mant, ex = np.frexp(amax / 6.0)
        byte = np.where(mant > 0.5, ex, ex - 1) + 127
    byte = np.clip(np.where(amax > 0, byte, 1), 1, 254)
    scaled = (w * np.exp2(127.0 - byte)[:, None, :]).reshape(k, n).astype(np.float32)
    by_word = np.ascontiguousarray(scaled.reshape(k // 512, 128, 4, n).transpose(0, 1, 3, 2))
    if fmt == "e4m3":
        words = by_word.astype(ml_dtypes.float8_e4m3fn).view(np.uint8)
    else:
        c = by_word.astype(ml_dtypes.float4_e2m1fn).view(np.uint8) & 0xF
        words = (c[..., 0::2] | (c[..., 1::2] << 4)).reshape(k // 512, 128, 2 * n)
    return np.ascontiguousarray(words), np.ascontiguousarray(byte.astype(np.uint8).reshape(k // 512, 16, n))


def unpack_weight(words, scales, fmt):
    g, _, n = scales.shape
    words = np.ascontiguousarray(words).reshape(g, 128, n, -1)
    if fmt == "e4m3":
        vals = words.view(ml_dtypes.float8_e4m3fn).astype(np.float64)
    else:
        nib = np.empty((g, 128, n, 4), np.uint8)
        nib[..., 0::2] = words & 0xF
        nib[..., 1::2] = words >> 4
        vals = E2M1[nib]
    vals = vals * np.repeat(np.exp2(scales.astype(np.float64) - 127.0), 8, axis=1)[..., None]
    return vals.transpose(0, 1, 3, 2).reshape(g * 512, n)


K, R, F, T, J, M = 512, 128, 512, 2048, 512, 256


def setup_inputs():
    n = np.random.standard_normal
    idx = np.random.permutation(T)[:J]
    idx2 = np.random.permutation(J)[:M]
    idx3 = np.random.permutation(J)[:M]
    idx4 = np.random.permutation(J)[:M]
    fk = mx_kscale(K)
    ff = mx_kscale(F)
    tabp = pack_weight(n((K, T)) / fk[:, None], "e4m3")
    dtabp = pack_weight(n((K, T)) / fk[:, None], "e4m3")
    return {
        "tab_words": tabp[0],
        "tab_scales": tabp[1],
        "w1": (n((K, R)) * 1 / np.sqrt(K) * fk[:, None]).astype(np.float32),
        "temper": (np.random.uniform(0.6, 2.0, (R, 1))).astype(np.float32),
        "wo": (n((F, R)) * 1 / np.sqrt(F) * ff[:, None]).astype(np.float32),
        "dy": (n((F, M)) / ff[:, None]).astype(np.float32),
        "dtab_words": dtabp[0],
        "dtab_scales": dtabp[1],
        "og": (np.random.uniform(0.7, 2.0, (R, 1))).astype(np.float32),
        "base": (0.3 * n((R, J))).astype(np.float32),
        "offs": striped(idx),
        "offs2": striped(idx2),
        "offs3": striped(idx3),
        "offs4": striped(idx4),
    }


def reference(tab_words, tab_scales, w1, temper, wo, dy, dtab_words, dtab_scales, og, base, offs, offs2, offs3, offs4):
    idx = unstriped(offs)
    idx2 = unstriped(offs2)
    idx3 = unstriped(offs3)
    idx4 = unstriped(offs4)
    tabu = unpack_weight(tab_words, tab_scales, "e4m3")
    dtabu = unpack_weight(dtab_words, dtab_scales, "e4m3")
    w1q = mxq(f64(w1), 0, "e4m3")
    tabidxg = tabu[:, idx]
    a = w1q.T @ tabidxg
    dtabidxg = dtabu[:, idx]
    ta = w1q.T @ dtabidxg
    e1s = np.exp(a * f64(temper) * (-1.0))
    s = e1s[:, idx2] + e1s[:, idx3] + e1s[:, idx4]
    woq = mxq(f64(wo), 0, "e4m3")
    dyq = mxq(f64(dy), 0, "e4m3")
    c0 = woq.T @ dyq
    ds = c0 * (-1.0) / f64(temper) / s
    s1 = np.zeros((R, J))
    s1[:, idx2] = ds
    s2 = np.zeros((R, J))
    s2[:, idx3] = ds
    s3 = np.zeros((R, J))
    s3[:, idx4] = ds
    de1s = s1 + s2 + s3
    xe1s = ta * f64(temper) * (-1.0) * e1s
    xs = xe1s[:, idx2] + xe1s[:, idx3] + xe1s[:, idx4]
    xds = xs * c0 * (-1.0) / f64(temper) / np.square(s) * (-1.0)
    xs1 = np.zeros((R, J))
    xs1[:, idx2] = xds
    xs2 = np.zeros((R, J))
    xs2[:, idx3] = xds
    xs3 = np.zeros((R, J))
    xs3[:, idx4] = xds
    xde1s = xs1 + xs2 + xs3
    xda = (xde1s * e1s + xe1s * de1s) * (-1.0) * f64(temper)
    y = xda * f64(og) + f64(base)
    return y

@@ -1,0 +1,182 @@
+from contextlib import ExitStack
+
+import concourse.mybir as mybir
+from concourse.masks import make_identity
+
+K, R, F, T, J, M = 512, 128, 512, 2048, 512, 256
+FLOPS = 2 * (2 * K * R * J + F * R * M)
+
+F32 = mybir.dt.float32
+BF16 = mybir.dt.bfloat16
+I32 = mybir.dt.int32
+U32 = mybir.dt.uint32
+U16 = mybir.dt.uint16
+U8 = mybir.dt.uint8
+FP8X4 = mybir.dt.float8_e4m3fn_x4
+ALU = mybir.AluOpType
+ACT = mybir.ActivationFunctionType
+
+P = 128
+PACK = 4
+HALF = J // 2
+
+
+def tile_attend_hvcsoftleast_kernel(
+    tc, tab_words, tab_scales, w1, temper, wo, dy, dtab_words, dtab_scales, og, base, offs, offs2, offs3, offs4, out
+):
+    nc = tc.nc
+    with ExitStack() as ctx:
+        lists = ctx.enter_context(tc.tile_pool(name="lists", bufs=1))
+        sb = ctx.enter_context(tc.tile_pool(name="sb", bufs=1))
+        ps = ctx.enter_context(tc.psum_pool(name="ps", bufs=1))
+
+        def load_list(src, n, name):
+            t = lists.tile([P, n // 16], U16, name=name)
+            nc.sync.dma_start(t[:], src)
+            return t
+
+        def load_scales(src, name, queue):
+            t = sb.tile([P, T], U8, name=name, tag=name, align_bytes=64)
+            nc.vector.memset(t[:].bitcast(I32), 0)
+            for q in range(4):
+                queue.dma_start(t[32 * q : 32 * q + 4, :].bitcast(I32), src[0, 4 * q : 4 * q + 4, :].bitcast(I32))
+            return t
+
+        def load_words(src, name, tag):
+            t = sb.tile([P, T], I32, name=name, tag=tag, align_bytes=64)
+            nc.sync.dma_start(t[:], src[0].rearrange("p n t -> p (n t)").bitcast(I32))
+            return t
+
+        def load_rows(src, width, name, tag):
+            t = sb.tile([P, PACK, width], F32, name=name, tag=tag, align_bytes=64)
+            nc.sync.dma_start(t[:], src.rearrange("(p t) w -> p t w", t=PACK))
+            return t
+
+        def load_column(src, name):
+            t = sb.tile([P, 1], F32, name=name)
+            nc.gpsimd.dma_start(t[:], src)
+            return t
+
+        def interleave(raw, width, name):
+            t = sb.tile([P, width, PACK], BF16, name=name, tag=name, align_bytes=64)
+            nc.scalar.copy(
+                t[:].rearrange("p (c i) t -> p c t i", i=4), raw[:].rearrange("p t (c i) -> p c t i", i=4)
+            )
+            return t
+
+        def quantize(grouped, width, name):
+            codes = sb.tile([P, width], U32, name=name + "_codes", align_bytes=64)
+            scales = sb.tile([P, width], U8, name=name + "_scales", align_bytes=64)
+            nc.vector.quantize_mx(
+                out=codes[:].bitcast(FP8X4), scales=scales[:], in_=grouped[:].rearrange("p w t -> p (w t)")
+            )
+            return codes, scales
+
+        def gather(window, offsets, n, dtype, name):
+            t = sb.tile([P, n], dtype, name=name, align_bytes=64)
+            nc.vector.tensor_copy(t[:], window.indirect(offsets[:]))
+            return t
+
+        def product(bank, lhs, rhs):
+            nc.tensor.matmul_mx(
+                out=bank, lhsT=lhs[0][:].bitcast(FP8X4), lhsT_scale=lhs[1][:],
+                rhs=rhs[0][:].bitcast(FP8X4), rhs_scale=rhs[1][:], start=True, stop=True,
+            )
+
+        slots = load_list(offs, J, "slots")
+        picks = [load_list(offs2, M, "picks0")]
+        w1_raw = load_rows(w1, R, "w1_raw", "w1_raw")
+        picks.append(load_list(offs3, M, "picks1"))
+        picks.append(load_list(offs4, M, "picks2"))
+        tab_w = load_words(tab_words, "tab_w", "tab_w")
+        tab_s = load_scales(tab_scales, "tab_s", nc.scalar)
+        dtab_s = load_scales(dtab_scales, "dtab_s", nc.sync)
+        temper_c = load_column(temper, "temper_c")
+        og_c = load_column(og, "og_c")
+
+        ident = sb.tile([P, P], F32, name="ident")
+        make_identity(nc, ident[:])
+        placed = [sb.tile([P, J], F32, name="placed%d" % i) for i in range(3)]
+        for t in placed:
+            nc.vector.memset(t[:], 0.0)
+
+        neg_temper = sb.tile([P, 1], F32, name="neg_temper")
+        nc.gpsimd.tensor_scalar(neg_temper[:], temper_c[:], -1.0, 0.0, ALU.mult, ALU.add)
+
+        w1_g = interleave(w1_raw, R, "w1_g")
+        tab_gs = gather(tab_s[:], slots, J, U8, "tab_gs")
+        w1_q = quantize(w1_g, R, "w1")
+        wo_raw = load_rows(wo, R, "wo_raw", "w1_raw")
+        dy_raw = load_rows(dy, M, "dy_raw", "tab_s")
+        dtab_w = load_words(dtab_words, "dtab_w", "w1_g")
+        tab_gw = gather(tab_w[:].bitcast(U32), slots, J, U32, "tab_gw")
+        base_sb = sb.tile([P, J], F32, name="base_sb", tag="tab_w", align_bytes=64)
+        nc.sync.dma_start(base_sb[:], base)
+        a_ps = ps.tile([P, J], F32, name="a_ps", tag="bank0")
+        product(a_ps[:], w1_q, (tab_gw, tab_gs))
+        wo_g = interleave(wo_raw, R, "wo_g")
+        dtab_gs = gather(dtab_s[:], slots, J, U8, "dtab_gs")
+        e = sb.tile([P, J], F32, name="e")
+        nc.scalar.activation(e[:], a_ps[:], ACT.Exp, scale=neg_temper[:])
+        dy_g = interleave(dy_raw, M, "dy_g")
+
+        e_p = [gather(e[:], picks[i], M, F32, "e_p%d" % i) for i in range(3)]
+        s01 = sb.tile([P, M], F32, name="s01")
+        s = sb.tile([P, M], F32, name="s")
+        nc.vector.tensor_tensor(s01[:], e_p[0][:], e_p[1][:], ALU.add)
+        nc.vector.tensor_tensor(s[:], s01[:], e_p[2][:], ALU.add)
+        root = sb.tile([P, M], F32, name="root")
+        inv_s = sb.tile([P, M], F32, name="inv_s")
+        nc.scalar.activation(root[:], s[:], ACT.Abs_reciprocal_sqrt)
+        nc.scalar.activation(inv_s[:], root[:], ACT.Square)
+
+        dtab_gw = gather(dtab_w[:].bitcast(U32), slots, J, U32, "dtab_gw")
+        ta_ps = ps.tile([P, J], F32, name="ta_ps", tag="bank1")
+        product(ta_ps[:], w1_q, (dtab_gw, dtab_gs))
+        wo_q = quantize(wo_g, R, "wo")
+        dy_q = quantize(dy_g, M, "dy")
+        c0_ps = ps.tile([P, M], F32, name="c0_ps", tag="bank2")
+        product(c0_ps[:], wo_q, dy_q)
+
+        xe = sb.tile([P, J], F32, name="xe")
+        nc.vector.scalar_tensor_tensor(xe[:], ta_ps[:], neg_temper[:], e[:], ALU.mult, ALU.mult)
+        g = sb.tile([P, M], F32, name="g")
+        nc.vector.scalar_tensor_tensor(g[:], c0_ps[:], og_c[:], inv_s[:], ALU.mult, ALU.mult)
+
+        gx = [sb.tile([P, M], F32, name="gx%d" % i) for i in range(3)]
+        for i in range(3):
+            nc.vector.tensor_tensor(gx[i][:], xe[:].indirect(picks[i][:]), g[:], ALU.mult)
+        gx01 = sb.tile([P, M], F32, name="gx01")
+        gxs = sb.tile([P, M], F32, name="gxs")
+        h = sb.tile([P, M], F32, name="h")
+        nc.vector.tensor_tensor(gx01[:], gx[0][:], gx[1][:], ALU.add)
+        nc.vector.tensor_tensor(gxs[:], gx01[:], gx[2][:], ALU.add)
+        nc.vector.scalar_tensor_tensor(h[:], gxs[:], -1.0, inv_s[:], ALU.mult, ALU.mult)
+
+        he = [sb.tile([P, M], F32, name="he%d" % i) for i in range(3)]
+        nc.vector.tensor_tensor(he[0][:], e_p[0][:], h[:], ALU.mult)
+        nc.vector.tensor_tensor(he[1][:], e_p[1][:], h[:], ALU.mult)
+        nc.vector.tensor_tensor(placed[0][:].indirect(picks[0][:]), gx[0][:], he[0][:], ALU.add)
+        nc.vector.tensor_tensor(placed[1][:].indirect(picks[1][:]), gx[1][:], he[1][:], ALU.add)
+        nc.vector.tensor_tensor(he[2][:], e_p[2][:], h[:], ALU.mult)
+        nc.vector.tensor_tensor(placed[2][:].indirect(picks[2][:]), gx[2][:], he[2][:], ALU.add)
+
+        blocks = J // P
+        turned = [ps.tile([P, P], F32, name="turned%d" % b, tag="bank%d" % (3 + b)) for b in range(blocks)]
+        terms = (base_sb, placed[0], placed[1])
+        for n, term in enumerate(terms):
+            for b in range(blocks):
+                nc.tensor.matmul(
+                    turned[b][:], term[:, b * P : (b + 1) * P], ident[:],
+                    start=(n == 0), stop=(n == len(terms) - 1), is_transpose=True,
+                )
+        turned_sb = [sb.tile([P, P], F32, name="turned_sb%d" % b) for b in range(blocks)]
+        back = [ps.tile([P, HALF], F32, name="back%d" % u, tag="bank%d" % u) for u in range(2)]
+        for b in range(blocks):
+            nc.scalar.copy(turned_sb[b][:], turned[b][:])
+            nc.tensor.transpose(back[b // 2][:, (b % 2) * P : (b % 2 + 1) * P], turned_sb[b][:], ident[:])
+        for u in range(2):
+            cols = slice(u * HALF, (u + 1) * HALF)
+            y = sb.tile([P, HALF], F32, name="y%d" % u)
+            nc.vector.tensor_tensor(y[:], back[u][:], placed[2][:, cols], ALU.add)
+            nc.sync.dma_start(out[:, cols], y[:])

@@ -1,7 +1,6 @@
 from contextlib import ExitStack
 
 import concourse.mybir as mybir
-from concourse.masks import make_identity
 
 K, R, F, T, J, M = 512, 128, 512, 2048, 512, 256
 FLOPS = 2 * (2 * K * R * J + F * R * M)
@@ -28,6 +27,7 @@ def tile_attend_hvcsoftleast_kernel(
     with ExitStack() as ctx:
         lists = ctx.enter_context(tc.tile_pool(name="lists", bufs=1))
         sb = ctx.enter_context(tc.tile_pool(name="sb", bufs=1))
+        shared = ctx.enter_context(tc.tile_pool(name="shared", bufs=1))
         ps = ctx.enter_context(tc.psum_pool(name="ps", bufs=1))
 
         def load_list(src, n, name):
@@ -35,45 +35,33 @@ def tile_attend_hvcsoftleast_kernel(
             nc.sync.dma_start(t[:], src)
             return t
 
-        def load_scales(src, name, queue):
-            t = sb.tile([P, T], U8, name=name, tag=name, align_bytes=64)
-            nc.vector.memset(t[:].bitcast(I32), 0)
-            for q in range(4):
+        def load_scales(t, src, queues):
+            for q, queue in enumerate(queues):
                 queue.dma_start(t[32 * q : 32 * q + 4, :].bitcast(I32), src[0, 4 * q : 4 * q + 4, :].bitcast(I32))
-            return t
 
-        def load_words(src, name, tag):
-            t = sb.tile([P, T], I32, name=name, tag=tag, align_bytes=64)
-            nc.sync.dma_start(t[:], src[0].rearrange("p n t -> p (n t)").bitcast(I32))
-            return t
+        def load_words(t, src, queue):
+            queue.dma_start(t[:], src[0].rearrange("p n t -> p (n t)").bitcast(I32))
 
         def load_rows(src, width, name, tag):
             t = sb.tile([P, PACK, width], F32, name=name, tag=tag, align_bytes=64)
             nc.sync.dma_start(t[:], src.rearrange("(p t) w -> p t w", t=PACK))
             return t
 
-        def load_column(src, name):
-            t = sb.tile([P, 1], F32, name=name)
-            nc.gpsimd.dma_start(t[:], src)
-            return t
-
-        def interleave(raw, width, name):
-            t = sb.tile([P, width, PACK], BF16, name=name, tag=name, align_bytes=64)
+        def interleave(t, raw):
             nc.scalar.copy(
                 t[:].rearrange("p (c i) t -> p c t i", i=4), raw[:].rearrange("p t (c i) -> p c t i", i=4)
             )
-            return t
 
-        def quantize(grouped, width, name):
-            codes = sb.tile([P, width], U32, name=name + "_codes", align_bytes=64)
+        def quantize(grouped, width, name, tag):
+            codes = sb.tile([P, width], U32, name=name + "_codes", tag=tag, align_bytes=64)
             scales = sb.tile([P, width], U8, name=name + "_scales", align_bytes=64)
             nc.vector.quantize_mx(
                 out=codes[:].bitcast(FP8X4), scales=scales[:], in_=grouped[:].rearrange("p w t -> p (w t)")
             )
             return codes, scales
 
-        def gather(window, offsets, n, dtype, name):
-            t = sb.tile([P, n], dtype, name=name, align_bytes=64)
+        def gather(window, offsets, n, dtype, name, tag=None):
+            t = sb.tile([P, n], dtype, name=name, tag=tag or name, align_bytes=64)
             nc.vector.tensor_copy(t[:], window.indirect(offsets[:]))
             return t
 
@@ -83,19 +71,29 @@ def tile_attend_hvcsoftleast_kernel(
                 rhs=rhs[0][:].bitcast(FP8X4), rhs_scale=rhs[1][:], start=True, stop=True,
             )
 
+        tab_s = sb.tile([P, T], U8, name="tab_s", tag="tab_s", align_bytes=64)
+        dtab_s = sb.tile([P, T], U8, name="dtab_s", tag="dtab_s", align_bytes=64)
+        zeros = shared.tile([P, P], F32, name="zeros", offset=768, align_bytes=64)
+        ident = sb.tile([P, P], F32, name="ident")
+        nc.vector.memset(tab_s[:].bitcast(I32), 0)
+        nc.vector.memset(dtab_s[:].bitcast(I32), 0)
+        nc.gpsimd.memset(zeros[:], 0.0)
+        nc.gpsimd.affine_select(
+            out=ident[:], in_=zeros[:], compare_op=ALU.not_equal, fill=1.0, base=0,
+            pattern=[[-1, P]], channel_multiplier=1,
+        )
         slots = load_list(offs, J, "slots")
         picks = [load_list(offs2, M, "picks0")]
         w1_raw = load_rows(w1, R, "w1_raw", "w1_raw")
-        picks.append(load_list(offs3, M, "picks1"))
-        picks.append(load_list(offs4, M, "picks2"))
-        tab_w = load_words(tab_words, "tab_w", "tab_w")
-        tab_s = load_scales(tab_scales, "tab_s", nc.scalar)
-        dtab_s = load_scales(dtab_scales, "dtab_s", nc.sync)
-        temper_c = load_column(temper, "temper_c")
-        og_c = load_column(og, "og_c")
-
-        ident = sb.tile([P, P], F32, name="ident")
-        make_identity(nc, ident[:])
+        picks += [load_list(offs3, M, "picks1"), load_list(offs4, M, "picks2")]
+        tab_w = sb.tile([P, T], I32, name="tab_w", tag="tab_w", align_bytes=64)
+        load_words(tab_w, tab_words, nc.sync)
+        load_scales(tab_s, tab_scales, [nc.scalar] * 4)
+        load_scales(dtab_s, dtab_scales, [nc.sync, nc.sync, nc.gpsimd, nc.gpsimd])
+        dtab_w = shared.tile([P, T], I32, name="dtab_w", offset=1024, align_bytes=64)
+        load_words(dtab_w, dtab_words, nc.sync)
+        temper_c = shared.tile([P, 1], F32, name="temper_c", offset=768, align_bytes=64)
+        nc.gpsimd.dma_start(temper_c[:], temper)
         placed = [sb.tile([P, J], F32, name="placed%d" % i) for i in range(3)]
         for t in placed:
             nc.vector.memset(t[:], 0.0)
@@ -103,38 +101,46 @@ def tile_attend_hvcsoftleast_kernel(
         neg_temper = sb.tile([P, 1], F32, name="neg_temper")
         nc.gpsimd.tensor_scalar(neg_temper[:], temper_c[:], -1.0, 0.0, ALU.mult, ALU.add)
 
-        w1_g = interleave(w1_raw, R, "w1_g")
+        w1_g = sb.tile([P, R, PACK], BF16, name="w1_g", align_bytes=64)
+        interleave(w1_g, w1_raw)
         tab_gs = gather(tab_s[:], slots, J, U8, "tab_gs")
-        w1_q = quantize(w1_g, R, "w1")
-        wo_raw = load_rows(wo, R, "wo_raw", "w1_raw")
+        w1_q = quantize(w1_g, R, "w1", "w1_codes")
         dy_raw = load_rows(dy, M, "dy_raw", "tab_s")
-        dtab_w = load_words(dtab_words, "dtab_w", "w1_g")
+        wo_raw = load_rows(wo, R, "wo_raw", "w1_raw")
         tab_gw = gather(tab_w[:].bitcast(U32), slots, J, U32, "tab_gw")
-        base_sb = sb.tile([P, J], F32, name="base_sb", tag="tab_w", align_bytes=64)
-        nc.sync.dma_start(base_sb[:], base)
         a_ps = ps.tile([P, J], F32, name="a_ps", tag="bank0")
         product(a_ps[:], w1_q, (tab_gw, tab_gs))
-        wo_g = interleave(wo_raw, R, "wo_g")
-        dtab_gs = gather(dtab_s[:], slots, J, U8, "dtab_gs")
+        dtab_gs = gather(dtab_s[:], slots, J, U8, "dtab_gs", "tab_w")
         e = sb.tile([P, J], F32, name="e")
         nc.scalar.activation(e[:], a_ps[:], ACT.Exp, scale=neg_temper[:])
-        dy_g = interleave(dy_raw, M, "dy_g")
+        warm = sb.tile([P, 1], F32, name="warm")
+        nc.scalar.activation(warm[:], e[:, 0:1], ACT.Abs_reciprocal_sqrt)
+        wo_g = sb.tile([P, R, PACK], BF16, name="wo_g", tag="tab_gw", align_bytes=64)
+        interleave(wo_g, wo_raw)
+        og_c = sb.tile([P, 1], F32, name="og_c", tag="w1_raw", align_bytes=64)
+        nc.sync.dma_start(og_c[:], og)
+        dy_g = sb.tile([P, M, PACK], BF16, name="dy_g", tag="tab_gs", align_bytes=64)
+        interleave(dy_g, dy_raw)
 
-        e_p = [gather(e[:], picks[i], M, F32, "e_p%d" % i) for i in range(3)]
-        s01 = sb.tile([P, M], F32, name="s01")
+        dtab_gw = gather(dtab_w[:].bitcast(U32), slots, J, U32, "dtab_gw", "dtab_s")
+        ta_ps = ps.tile([P, J], F32, name="ta_ps", tag="bank1")
+        product(ta_ps[:], w1_q, (dtab_gw, dtab_gs))
+        base_sb = sb.tile([P, J], F32, name="base_sb", tag="tab_w", align_bytes=64)
+        nc.sync.dma_start(base_sb[:], base)
+        e_p = shared.tile([P, 3, M], F32, name="e_p", offset=1024, align_bytes=64)
+        for i in range(3):
+            nc.vector.tensor_copy(e_p[:, i, :], e[:].indirect(picks[i][:]))
+        s01 = sb.tile([P, M], F32, name="s01", tag="s01", align_bytes=64)
         s = sb.tile([P, M], F32, name="s")
-        nc.vector.tensor_tensor(s01[:], e_p[0][:], e_p[1][:], ALU.add)
-        nc.vector.tensor_tensor(s[:], s01[:], e_p[2][:], ALU.add)
+        nc.vector.tensor_tensor(s01[:], e_p[:, 0, :], e_p[:, 1, :], ALU.add)
+        nc.vector.tensor_tensor(s[:], s01[:], e_p[:, 2, :], ALU.add)
         root = sb.tile([P, M], F32, name="root")
         inv_s = sb.tile([P, M], F32, name="inv_s")
         nc.scalar.activation(root[:], s[:], ACT.Abs_reciprocal_sqrt)
         nc.scalar.activation(inv_s[:], root[:], ACT.Square)
 
-        dtab_gw = gather(dtab_w[:].bitcast(U32), slots, J, U32, "dtab_gw")
-        ta_ps = ps.tile([P, J], F32, name="ta_ps", tag="bank1")
-        product(ta_ps[:], w1_q, (dtab_gw, dtab_gs))
-        wo_q = quantize(wo_g, R, "wo")
-        dy_q = quantize(dy_g, M, "dy")
+        wo_q = quantize(wo_g, R, "wo", "dtab_s")
+        dy_q = quantize(dy_g, M, "dy", "s01")
         c0_ps = ps.tile([P, M], F32, name="c0_ps", tag="bank2")
         product(c0_ps[:], wo_q, dy_q)
 
@@ -154,29 +160,30 @@ def tile_attend_hvcsoftleast_kernel(
         nc.vector.scalar_tensor_tensor(h[:], gxs[:], -1.0, inv_s[:], ALU.mult, ALU.mult)
 
         he = [sb.tile([P, M], F32, name="he%d" % i) for i in range(3)]
-        nc.vector.tensor_tensor(he[0][:], e_p[0][:], h[:], ALU.mult)
-        nc.vector.tensor_tensor(he[1][:], e_p[1][:], h[:], ALU.mult)
+        nc.vector.tensor_tensor(he[0][:], e_p[:, 0, :], h[:], ALU.mult)
+        nc.vector.tensor_tensor(he[1][:], e_p[:, 1, :], h[:], ALU.mult)
         nc.vector.tensor_tensor(placed[0][:].indirect(picks[0][:]), gx[0][:], he[0][:], ALU.add)
         nc.vector.tensor_tensor(placed[1][:].indirect(picks[1][:]), gx[1][:], he[1][:], ALU.add)
-        nc.vector.tensor_tensor(he[2][:], e_p[2][:], h[:], ALU.mult)
+        nc.vector.tensor_tensor(he[2][:], e_p[:, 2, :], h[:], ALU.mult)
         nc.vector.tensor_tensor(placed[2][:].indirect(picks[2][:]), gx[2][:], he[2][:], ALU.add)
 
         blocks = J // P
         turned = [ps.tile([P, P], F32, name="turned%d" % b, tag="bank%d" % (3 + b)) for b in range(blocks)]
-        terms = (base_sb, placed[0], placed[1])
-        for n, term in enumerate(terms):
-            for b in range(blocks):
-                nc.tensor.matmul(
-                    turned[b][:], term[:, b * P : (b + 1) * P], ident[:],
-                    start=(n == 0), stop=(n == len(terms) - 1), is_transpose=True,
-                )
+        terms = [(base_sb, placed[0], placed[1]) if b < 2 else (base_sb, placed[0]) for b in range(blocks)]
         turned_sb = [sb.tile([P, P], F32, name="turned_sb%d" % b) for b in range(blocks)]
         back = [ps.tile([P, HALF], F32, name="back%d" % u, tag="bank%d" % u) for u in range(2)]
-        for b in range(blocks):
+        for b in (2, 3, 0, 1):
+            for n, term in enumerate(terms[b]):
+                nc.tensor.matmul(
+                    turned[b][:], term[:, b * P : (b + 1) * P], ident[:],
+                    start=(n == 0), stop=(n == len(terms[b]) - 1), is_transpose=True,
+                )
             nc.scalar.copy(turned_sb[b][:], turned[b][:])
             nc.tensor.transpose(back[b // 2][:, (b % 2) * P : (b % 2 + 1) * P], turned_sb[b][:], ident[:])
-        for u in range(2):
+        upper = sb.tile([P, HALF], F32, name="upper")
+        nc.vector.tensor_tensor(upper[:], back[1][:], placed[1][:, HALF:], ALU.add)
+        for u, part in ((1, upper), (0, back[0])):
             cols = slice(u * HALF, (u + 1) * HALF)
             y = sb.tile([P, HALF], F32, name="y%d" % u)
-            nc.vector.tensor_tensor(y[:], back[u][:], placed[2][:, cols], ALU.add)
+            nc.vector.tensor_tensor(y[:], part[:], placed[2][:, cols], ALU.add)
             nc.sync.dma_start(out[:, cols], y[:])

@@ -27,7 +27,7 @@ def tile_attend_hvcsoftleast_kernel(
     with ExitStack() as ctx:
         lists = ctx.enter_context(tc.tile_pool(name="lists", bufs=1))
         sb = ctx.enter_context(tc.tile_pool(name="sb", bufs=1))
-        shared = ctx.enter_context(tc.tile_pool(name="shared", bufs=1))
+        late = ctx.enter_context(tc.tile_pool(name="late", bufs=1))
         ps = ctx.enter_context(tc.psum_pool(name="ps", bufs=1))
 
         def load_list(src, n, name):
@@ -42,14 +42,12 @@ def tile_attend_hvcsoftleast_kernel(
         def load_words(t, src, queue):
             queue.dma_start(t[:], src[0].rearrange("p n t -> p (n t)").bitcast(I32))
 
-        def load_rows(src, width, name, tag):
-            t = sb.tile([P, PACK, width], F32, name=name, tag=tag, align_bytes=64)
+        def load_rows(t, src):
             nc.sync.dma_start(t[:], src.rearrange("(p t) w -> p t w", t=PACK))
-            return t
 
         def interleave(t, raw):
             nc.scalar.copy(
-                t[:].rearrange("p (c i) t -> p c t i", i=4), raw[:].rearrange("p t (c i) -> p c t i", i=4)
+                t.rearrange("p (c i) t -> p c t i", i=4), raw[:].rearrange("p t (c i) -> p c t i", i=4)
             )
 
         def quantize(grouped, width, name, tag):
@@ -67,87 +65,99 @@ def tile_attend_hvcsoftleast_kernel(
 
         def product(bank, lhs, rhs):
             nc.tensor.matmul_mx(
-                out=bank, lhsT=lhs[0][:].bitcast(FP8X4), lhsT_scale=lhs[1][:],
-                rhs=rhs[0][:].bitcast(FP8X4), rhs_scale=rhs[1][:], start=True, stop=True,
+                out=bank, lhsT=lhs[0].bitcast(FP8X4), lhsT_scale=lhs[1],
+                rhs=rhs[0].bitcast(FP8X4), rhs_scale=rhs[1], start=True, stop=True,
             )
 
-        tab_s = sb.tile([P, T], U8, name="tab_s", tag="tab_s", align_bytes=64)
+        tab_s = sb.tile([P, T], U8, name="tab_s", align_bytes=64)
         dtab_s = sb.tile([P, T], U8, name="dtab_s", tag="dtab_s", align_bytes=64)
-        zeros = shared.tile([P, P], F32, name="zeros", offset=768, align_bytes=64)
+        placed = [sb.tile([P, J], F32, name="placed%d" % i) for i in range(3)]
+        zeros = late.tile([P, 4096], F32, name="zeros", offset=0, align_bytes=64)
         ident = sb.tile([P, P], F32, name="ident")
         nc.vector.memset(tab_s[:].bitcast(I32), 0)
+        nc.vector.memset(placed[0][:], 0.0)
+        nc.vector.memset(placed[1][:], 0.0)
         nc.vector.memset(dtab_s[:].bitcast(I32), 0)
-        nc.gpsimd.memset(zeros[:], 0.0)
+        nc.vector.memset(zeros[:, :P], 0.0)
+        nc.vector.memset(placed[2][:], 0.0)
+        slots = load_list(offs, J, "slots")
+        tab_w = sb.tile([P, T], I32, name="tab_w", align_bytes=64)
+        load_words(tab_w, tab_words, nc.scalar)
+        warm = sb.tile([P, 1], F32, name="warm")
+        nc.scalar.activation(warm[:], placed[0][:, 0:1], ACT.Exp)
+        w1_raw = sb.tile([P, PACK, R], F32, name="w1_raw")
+        load_rows(w1_raw, w1)
+        picks = [load_list(src, M, "picks%d" % i) for i, src in enumerate((offs2, offs3, offs4))]
+        load_scales(tab_s, tab_scales, [nc.sync, nc.sync, nc.sync, nc.gpsimd])
         nc.gpsimd.affine_select(
-            out=ident[:], in_=zeros[:], compare_op=ALU.not_equal, fill=1.0, base=0,
+            out=ident[:], in_=zeros[:, :P], compare_op=ALU.not_equal, fill=1.0, base=0,
             pattern=[[-1, P]], channel_multiplier=1,
         )
-        slots = load_list(offs, J, "slots")
-        picks = [load_list(offs2, M, "picks0")]
-        w1_raw = load_rows(w1, R, "w1_raw", "w1_raw")
-        picks += [load_list(offs3, M, "picks1"), load_list(offs4, M, "picks2")]
-        tab_w = sb.tile([P, T], I32, name="tab_w", tag="tab_w", align_bytes=64)
-        load_words(tab_w, tab_words, nc.sync)
-        load_scales(tab_s, tab_scales, [nc.scalar] * 4)
-        load_scales(dtab_s, dtab_scales, [nc.sync, nc.sync, nc.gpsimd, nc.gpsimd])
-        dtab_w = shared.tile([P, T], I32, name="dtab_w", offset=1024, align_bytes=64)
-        load_words(dtab_w, dtab_words, nc.sync)
-        temper_c = shared.tile([P, 1], F32, name="temper_c", offset=768, align_bytes=64)
+        load_scales(dtab_s, dtab_scales, [nc.sync, nc.scalar, nc.sync, nc.scalar])
+        temper_c = late.tile([P, 1], F32, name="temper_c", offset=6144, align_bytes=64)
         nc.gpsimd.dma_start(temper_c[:], temper)
-        placed = [sb.tile([P, J], F32, name="placed%d" % i) for i in range(3)]
-        for t in placed:
-            nc.vector.memset(t[:], 0.0)
+        wo_raw = late.tile([P, PACK, R], F32, name="wo_raw", offset=0, align_bytes=64)
+        load_rows(wo_raw, wo)
+        dy_raw = late.tile([P, PACK, M], F32, name="dy_raw", offset=2048, align_bytes=64)
+        load_rows(dy_raw, dy)
+        dtab_w = late.tile([P, T], I32, name="dtab_w", offset=8320, align_bytes=64)
+        load_words(dtab_w, dtab_words, nc.sync)
+        og_c = late.tile([P, 1], F32, name="og_c", offset=6208, align_bytes=64)
+        nc.sync.dma_start(og_c[:], og)
+        base_sb = late.tile([P, J], F32, name="base_sb", offset=6272, align_bytes=64)
+        nc.sync.dma_start(base_sb[:], base)
 
         neg_temper = sb.tile([P, 1], F32, name="neg_temper")
         nc.gpsimd.tensor_scalar(neg_temper[:], temper_c[:], -1.0, 0.0, ALU.mult, ALU.add)
 
-        w1_g = sb.tile([P, R, PACK], BF16, name="w1_g", align_bytes=64)
-        interleave(w1_g, w1_raw)
-        tab_gs = gather(tab_s[:], slots, J, U8, "tab_gs")
-        w1_q = quantize(w1_g, R, "w1", "w1_codes")
-        dy_raw = load_rows(dy, M, "dy_raw", "tab_s")
-        wo_raw = load_rows(wo, R, "wo_raw", "w1_raw")
+        w1_g = sb.tile([P, R, PACK], BF16, name="w1_g", tag="w_g", align_bytes=64)
+        interleave(w1_g[:], w1_raw)
         tab_gw = gather(tab_w[:].bitcast(U32), slots, J, U32, "tab_gw")
+        tab_gs = gather(tab_s[:], slots, J, U8, "tab_gs")
+        w1_codes, w1_scales = quantize(w1_g, R, "w1", "w1_codes")
+        w1_q = (w1_codes[:], w1_scales[:])
         a_ps = ps.tile([P, J], F32, name="a_ps", tag="bank0")
-        product(a_ps[:], w1_q, (tab_gw, tab_gs))
-        dtab_gs = gather(dtab_s[:], slots, J, U8, "dtab_gs", "tab_w")
+        product(a_ps[:], w1_q, (tab_gw[:], tab_gs[:]))
+        dtab_gs = gather(dtab_s[:], slots, J, U8, "dtab_gs", "w_g")
+        wo_g = sb.tile([P, R, PACK], BF16, name="wo_g", align_bytes=64)
+        interleave(wo_g[:], wo_raw)
+        wo_codes, wo_scales = quantize(wo_g, R, "wo", "wo_codes")
         e = sb.tile([P, J], F32, name="e")
         nc.scalar.activation(e[:], a_ps[:], ACT.Exp, scale=neg_temper[:])
-        warm = sb.tile([P, 1], F32, name="warm")
-        nc.scalar.activation(warm[:], e[:, 0:1], ACT.Abs_reciprocal_sqrt)
-        wo_g = sb.tile([P, R, PACK], BF16, name="wo_g", tag="tab_gw", align_bytes=64)
-        interleave(wo_g, wo_raw)
-        og_c = sb.tile([P, 1], F32, name="og_c", tag="w1_raw", align_bytes=64)
-        nc.sync.dma_start(og_c[:], og)
         dy_g = sb.tile([P, M, PACK], BF16, name="dy_g", tag="tab_gs", align_bytes=64)
-        interleave(dy_g, dy_raw)
+        interleave(dy_g[:], dy_raw)
 
-        dtab_gw = gather(dtab_w[:].bitcast(U32), slots, J, U32, "dtab_gw", "dtab_s")
-        ta_ps = ps.tile([P, J], F32, name="ta_ps", tag="bank1")
-        product(ta_ps[:], w1_q, (dtab_gw, dtab_gs))
-        base_sb = sb.tile([P, J], F32, name="base_sb", tag="tab_w", align_bytes=64)
-        nc.sync.dma_start(base_sb[:], base)
-        e_p = shared.tile([P, 3, M], F32, name="e_p", offset=1024, align_bytes=64)
+        e_p = sb.tile([P, 3, M], F32, name="e_p", tag="dtab_s", align_bytes=64)
         for i in range(3):
             nc.vector.tensor_copy(e_p[:, i, :], e[:].indirect(picks[i][:]))
-        s01 = sb.tile([P, M], F32, name="s01", tag="s01", align_bytes=64)
-        s = sb.tile([P, M], F32, name="s")
-        nc.vector.tensor_tensor(s01[:], e_p[:, 0, :], e_p[:, 1, :], ALU.add)
-        nc.vector.tensor_tensor(s[:], s01[:], e_p[:, 2, :], ALU.add)
         root = sb.tile([P, M], F32, name="root")
-        inv_s = sb.tile([P, M], F32, name="inv_s")
-        nc.scalar.activation(root[:], s[:], ACT.Abs_reciprocal_sqrt)
-        nc.scalar.activation(inv_s[:], root[:], ACT.Square)
+        for u, bank in enumerate(("bank7", "bank0")):
+            s_turned = ps.tile([P, P], F32, name="s_turned%d" % u, tag=bank)
+            for i in range(3):
+                nc.tensor.matmul(
+                    s_turned[:], e_p[:, i, u * P : (u + 1) * P], ident[:],
+                    start=(i == 0), stop=(i == 2), is_transpose=True,
+                )
+            nc.scalar.activation(root[:, u * P : (u + 1) * P], s_turned[:], ACT.Abs_reciprocal_sqrt)
+        inv_s_turned = sb.tile([P, M], F32, name="inv_s_turned")
+        nc.scalar.activation(inv_s_turned[:], root[:], ACT.Square)
+        inv_s = ps.tile([P, M], F32, name="inv_s", tag="bank3")
+        for u in range(2):
+            nc.tensor.transpose(inv_s[:, u * P : (u + 1) * P], inv_s_turned[:, u * P : (u + 1) * P], ident[:])
 
-        wo_q = quantize(wo_g, R, "wo", "dtab_s")
-        dy_q = quantize(dy_g, M, "dy", "s01")
+        dtab_gw = gather(dtab_w[:].bitcast(U32), slots, J, U32, "dtab_gw")
+        ta_ps = ps.tile([P, J], F32, name="ta_ps", tag="bank1")
+        product(ta_ps[:], w1_q, (dtab_gw[:], dtab_gs[:]))
+        dy_codes, dy_scales = quantize(dy_g, M, "dy", "dy_codes")
         c0_ps = ps.tile([P, M], F32, name="c0_ps", tag="bank2")
-        product(c0_ps[:], wo_q, dy_q)
+        product(c0_ps[:], (wo_codes[:], wo_scales[:]), (dy_codes[:], dy_scales[:]))
+        c0_og = sb.tile([P, M], F32, name="c0_og")
+        nc.scalar.activation(c0_og[:], c0_ps[:], ACT.Copy, scale=og_c[:])
 
         xe = sb.tile([P, J], F32, name="xe")
         nc.vector.scalar_tensor_tensor(xe[:], ta_ps[:], neg_temper[:], e[:], ALU.mult, ALU.mult)
         g = sb.tile([P, M], F32, name="g")
-        nc.vector.scalar_tensor_tensor(g[:], c0_ps[:], og_c[:], inv_s[:], ALU.mult, ALU.mult)
+        nc.vector.tensor_tensor(g[:], inv_s[:], c0_og[:], ALU.mult)
 
         gx = [sb.tile([P, M], F32, name="gx%d" % i) for i in range(3)]
         for i in range(3):
@@ -157,7 +167,7 @@ def tile_attend_hvcsoftleast_kernel(
         h = sb.tile([P, M], F32, name="h")
         nc.vector.tensor_tensor(gx01[:], gx[0][:], gx[1][:], ALU.add)
         nc.vector.tensor_tensor(gxs[:], gx01[:], gx[2][:], ALU.add)
-        nc.vector.scalar_tensor_tensor(h[:], gxs[:], -1.0, inv_s[:], ALU.mult, ALU.mult)
+        nc.vector.scalar_tensor_tensor(h[:], inv_s[:], -1.0, gxs[:], ALU.mult, ALU.mult)
 
         he = [sb.tile([P, M], F32, name="he%d" % i) for i in range(3)]
         nc.vector.tensor_tensor(he[0][:], e_p[:, 0, :], h[:], ALU.mult)
@@ -169,21 +179,20 @@ def tile_attend_hvcsoftleast_kernel(
 
         blocks = J // P
         turned = [ps.tile([P, P], F32, name="turned%d" % b, tag="bank%d" % (3 + b)) for b in range(blocks)]
-        terms = [(base_sb, placed[0], placed[1]) if b < 2 else (base_sb, placed[0]) for b in range(blocks)]
-        turned_sb = [sb.tile([P, P], F32, name="turned_sb%d" % b) for b in range(blocks)]
-        back = [ps.tile([P, HALF], F32, name="back%d" % u, tag="bank%d" % u) for u in range(2)]
-        for b in (2, 3, 0, 1):
-            for n, term in enumerate(terms[b]):
+        terms = (base_sb, placed[0], placed[1])
+        for n, term in enumerate(terms):
+            for b in range(blocks):
                 nc.tensor.matmul(
                     turned[b][:], term[:, b * P : (b + 1) * P], ident[:],
-                    start=(n == 0), stop=(n == len(terms[b]) - 1), is_transpose=True,
+                    start=(n == 0), stop=(n == len(terms) - 1), is_transpose=True,
                 )
+        turned_sb = [sb.tile([P, P], F32, name="turned_sb%d" % b) for b in range(blocks)]
+        back = [ps.tile([P, HALF], F32, name="back%d" % u, tag="bank%d" % u) for u in range(2)]
+        for b in range(blocks):
             nc.scalar.copy(turned_sb[b][:], turned[b][:])
             nc.tensor.transpose(back[b // 2][:, (b % 2) * P : (b % 2 + 1) * P], turned_sb[b][:], ident[:])
-        upper = sb.tile([P, HALF], F32, name="upper")
-        nc.vector.tensor_tensor(upper[:], back[1][:], placed[1][:, HALF:], ALU.add)
-        for u, part in ((1, upper), (0, back[0])):
+        for u in range(2):
             cols = slice(u * HALF, (u + 1) * HALF)
             y = sb.tile([P, HALF], F32, name="y%d" % u)
-            nc.vector.tensor_tensor(y[:], part[:], placed[2][:, cols], ALU.add)
+            nc.vector.tensor_tensor(y[:], back[u][:], placed[2][:, cols], ALU.add)
             nc.sync.dma_start(out[:, cols], y[:])

from contextlib import ExitStack

import concourse.mybir as mybir

K, R, F, T, J, M = 512, 128, 512, 2048, 512, 256
FLOPS = 2 * (2 * K * R * J + F * R * M)

F32 = mybir.dt.float32
BF16 = mybir.dt.bfloat16
I32 = mybir.dt.int32
U32 = mybir.dt.uint32
U16 = mybir.dt.uint16
U8 = mybir.dt.uint8
FP8X4 = mybir.dt.float8_e4m3fn_x4
ALU = mybir.AluOpType
ACT = mybir.ActivationFunctionType

P = 128
PACK = 4
HALF = J // 2


def tile_attend_hvcsoftleast_kernel(
    tc, tab_words, tab_scales, w1, temper, wo, dy, dtab_words, dtab_scales, og, base, offs, offs2, offs3, offs4, out
):
    nc = tc.nc
    with ExitStack() as ctx:
        lists = ctx.enter_context(tc.tile_pool(name="lists", bufs=1))
        sb = ctx.enter_context(tc.tile_pool(name="sb", bufs=1))
        late = ctx.enter_context(tc.tile_pool(name="late", bufs=1))
        ps = ctx.enter_context(tc.psum_pool(name="ps", bufs=1))

        def load_list(src, n, name):
            t = lists.tile([P, n // 16], U16, name=name)
            nc.sync.dma_start(t[:], src)
            return t

        def load_scales(t, src, queues):
            for q, queue in enumerate(queues):
                queue.dma_start(t[32 * q : 32 * q + 4, :].bitcast(I32), src[0, 4 * q : 4 * q + 4, :].bitcast(I32))

        def load_words(t, src, queue):
            queue.dma_start(t[:], src[0].rearrange("p n t -> p (n t)").bitcast(I32))

        def load_rows(t, src):
            nc.sync.dma_start(t[:], src.rearrange("(p t) w -> p t w", t=PACK))

        def interleave(t, raw):
            nc.scalar.copy(
                t.rearrange("p (c i) t -> p c t i", i=4), raw[:].rearrange("p t (c i) -> p c t i", i=4)
            )

        def quantize(grouped, width, name, tag):
            codes = sb.tile([P, width], U32, name=name + "_codes", tag=tag, align_bytes=64)
            scales = sb.tile([P, width], U8, name=name + "_scales", align_bytes=64)
            nc.vector.quantize_mx(
                out=codes[:].bitcast(FP8X4), scales=scales[:], in_=grouped[:].rearrange("p w t -> p (w t)")
            )
            return codes, scales

        def gather(window, offsets, n, dtype, name, tag=None):
            t = sb.tile([P, n], dtype, name=name, tag=tag or name, align_bytes=64)
            nc.vector.tensor_copy(t[:], window.indirect(offsets[:]))
            return t

        def product(bank, lhs, rhs):
            nc.tensor.matmul_mx(
                out=bank, lhsT=lhs[0].bitcast(FP8X4), lhsT_scale=lhs[1],
                rhs=rhs[0].bitcast(FP8X4), rhs_scale=rhs[1], start=True, stop=True,
            )

        tab_s = sb.tile([P, T], U8, name="tab_s", align_bytes=64)
        dtab_s = sb.tile([P, T], U8, name="dtab_s", tag="dtab_s", align_bytes=64)
        placed = [sb.tile([P, J], F32, name="placed%d" % i) for i in range(3)]
        zeros = late.tile([P, 4096], F32, name="zeros", offset=0, align_bytes=64)
        ident = sb.tile([P, P], F32, name="ident")
        nc.vector.memset(tab_s[:].bitcast(I32), 0)
        nc.vector.memset(placed[0][:], 0.0)
        nc.vector.memset(placed[1][:], 0.0)
        nc.vector.memset(dtab_s[:].bitcast(I32), 0)
        nc.vector.memset(zeros[:, :P], 0.0)
        nc.vector.memset(placed[2][:], 0.0)
        slots = load_list(offs, J, "slots")
        tab_w = sb.tile([P, T], I32, name="tab_w", align_bytes=64)
        load_words(tab_w, tab_words, nc.scalar)
        warm = sb.tile([P, 1], F32, name="warm")
        nc.scalar.activation(warm[:], placed[0][:, 0:1], ACT.Exp)
        w1_raw = sb.tile([P, PACK, R], F32, name="w1_raw")
        load_rows(w1_raw, w1)
        picks = [load_list(src, M, "picks%d" % i) for i, src in enumerate((offs2, offs3, offs4))]
        load_scales(tab_s, tab_scales, [nc.sync, nc.sync, nc.sync, nc.gpsimd])
        nc.gpsimd.affine_select(
            out=ident[:], in_=zeros[:, :P], compare_op=ALU.not_equal, fill=1.0, base=0,
            pattern=[[-1, P]], channel_multiplier=1,
        )
        load_scales(dtab_s, dtab_scales, [nc.sync, nc.scalar, nc.sync, nc.scalar])
        temper_c = late.tile([P, 1], F32, name="temper_c", offset=6144, align_bytes=64)
        nc.gpsimd.dma_start(temper_c[:], temper)
        wo_raw = late.tile([P, PACK, R], F32, name="wo_raw", offset=0, align_bytes=64)
        load_rows(wo_raw, wo)
        dy_raw = late.tile([P, PACK, M], F32, name="dy_raw", offset=2048, align_bytes=64)
        load_rows(dy_raw, dy)
        dtab_w = late.tile([P, T], I32, name="dtab_w", offset=8320, align_bytes=64)
        load_words(dtab_w, dtab_words, nc.sync)
        og_c = late.tile([P, 1], F32, name="og_c", offset=6208, align_bytes=64)
        nc.sync.dma_start(og_c[:], og)
        base_sb = late.tile([P, J], F32, name="base_sb", offset=6272, align_bytes=64)
        nc.sync.dma_start(base_sb[:], base)

        neg_temper = sb.tile([P, 1], F32, name="neg_temper")
        nc.gpsimd.tensor_scalar(neg_temper[:], temper_c[:], -1.0, 0.0, ALU.mult, ALU.add)

        w1_g = sb.tile([P, R, PACK], BF16, name="w1_g", tag="w_g", align_bytes=64)
        interleave(w1_g[:], w1_raw)
        tab_gw = gather(tab_w[:].bitcast(U32), slots, J, U32, "tab_gw")
        tab_gs = gather(tab_s[:], slots, J, U8, "tab_gs")
        w1_codes, w1_scales = quantize(w1_g, R, "w1", "w1_codes")
        w1_q = (w1_codes[:], w1_scales[:])
        a_ps = ps.tile([P, J], F32, name="a_ps", tag="bank0")
        product(a_ps[:], w1_q, (tab_gw[:], tab_gs[:]))
        dtab_gs = gather(dtab_s[:], slots, J, U8, "dtab_gs", "w_g")
        wo_g = sb.tile([P, R, PACK], BF16, name="wo_g", align_bytes=64)
        interleave(wo_g[:], wo_raw)
        wo_codes, wo_scales = quantize(wo_g, R, "wo", "wo_codes")
        e = sb.tile([P, J], F32, name="e")
        nc.scalar.activation(e[:], a_ps[:], ACT.Exp, scale=neg_temper[:])
        dy_g = sb.tile([P, M, PACK], BF16, name="dy_g", tag="tab_gs", align_bytes=64)
        interleave(dy_g[:], dy_raw)

        e_p = sb.tile([P, 3, M], F32, name="e_p", tag="dtab_s", align_bytes=64)
        for i in range(3):
            nc.vector.tensor_copy(e_p[:, i, :], e[:].indirect(picks[i][:]))
        root = sb.tile([P, M], F32, name="root")
        for u, bank in enumerate(("bank7", "bank0")):
            s_turned = ps.tile([P, P], F32, name="s_turned%d" % u, tag=bank)
            for i in range(3):
                nc.tensor.matmul(
                    s_turned[:], e_p[:, i, u * P : (u + 1) * P], ident[:],
                    start=(i == 0), stop=(i == 2), is_transpose=True,
                )
            nc.scalar.activation(root[:, u * P : (u + 1) * P], s_turned[:], ACT.Abs_reciprocal_sqrt)
        inv_s_turned = sb.tile([P, M], F32, name="inv_s_turned")
        nc.scalar.activation(inv_s_turned[:], root[:], ACT.Square)
        inv_s = ps.tile([P, M], F32, name="inv_s", tag="bank3")
        for u in range(2):
            nc.tensor.transpose(inv_s[:, u * P : (u + 1) * P], inv_s_turned[:, u * P : (u + 1) * P], ident[:])

        dtab_gw = gather(dtab_w[:].bitcast(U32), slots, J, U32, "dtab_gw")
        ta_ps = ps.tile([P, J], F32, name="ta_ps", tag="bank1")
        product(ta_ps[:], w1_q, (dtab_gw[:], dtab_gs[:]))
        dy_codes, dy_scales = quantize(dy_g, M, "dy", "dy_codes")
        c0_ps = ps.tile([P, M], F32, name="c0_ps", tag="bank2")
        product(c0_ps[:], (wo_codes[:], wo_scales[:]), (dy_codes[:], dy_scales[:]))
        c0_og = sb.tile([P, M], F32, name="c0_og")
        nc.scalar.activation(c0_og[:], c0_ps[:], ACT.Copy, scale=og_c[:])

        xe = sb.tile([P, J], F32, name="xe")
        nc.vector.scalar_tensor_tensor(xe[:], ta_ps[:], neg_temper[:], e[:], ALU.mult, ALU.mult)
        g = sb.tile([P, M], F32, name="g")
        nc.vector.tensor_tensor(g[:], inv_s[:], c0_og[:], ALU.mult)

        gx = [sb.tile([P, M], F32, name="gx%d" % i) for i in range(3)]
        for i in range(3):
            nc.vector.tensor_tensor(gx[i][:], xe[:].indirect(picks[i][:]), g[:], ALU.mult)
        gx01 = sb.tile([P, M], F32, name="gx01")
        gxs = sb.tile([P, M], F32, name="gxs")
        h = sb.tile([P, M], F32, name="h")
        nc.vector.tensor_tensor(gx01[:], gx[0][:], gx[1][:], ALU.add)
        nc.vector.tensor_tensor(gxs[:], gx01[:], gx[2][:], ALU.add)
        nc.vector.scalar_tensor_tensor(h[:], inv_s[:], -1.0, gxs[:], ALU.mult, ALU.mult)

        he = [sb.tile([P, M], F32, name="he%d" % i) for i in range(3)]
        nc.vector.tensor_tensor(he[0][:], e_p[:, 0, :], h[:], ALU.mult)
        nc.vector.tensor_tensor(he[1][:], e_p[:, 1, :], h[:], ALU.mult)
        nc.vector.tensor_tensor(placed[0][:].indirect(picks[0][:]), gx[0][:], he[0][:], ALU.add)
        nc.vector.tensor_tensor(placed[1][:].indirect(picks[1][:]), gx[1][:], he[1][:], ALU.add)
        nc.vector.tensor_tensor(he[2][:], e_p[:, 2, :], h[:], ALU.mult)
        nc.vector.tensor_tensor(placed[2][:].indirect(picks[2][:]), gx[2][:], he[2][:], ALU.add)

        blocks = J // P
        turned = [ps.tile([P, P], F32, name="turned%d" % b, tag="bank%d" % (3 + b)) for b in range(blocks)]
        terms = (base_sb, placed[0], placed[1])
        for n, term in enumerate(terms):
            for b in range(blocks):
                nc.tensor.matmul(
                    turned[b][:], term[:, b * P : (b + 1) * P], ident[:],
                    start=(n == 0), stop=(n == len(terms) - 1), is_transpose=True,
                )
        turned_sb = [sb.tile([P, P], F32, name="turned_sb%d" % b) for b in range(blocks)]
        back = [ps.tile([P, HALF], F32, name="back%d" % u, tag="bank%d" % u) for u in range(2)]
        for b in range(blocks):
            nc.scalar.copy(turned_sb[b][:], turned[b][:])
            nc.tensor.transpose(back[b // 2][:, (b % 2) * P : (b % 2 + 1) * P], turned_sb[b][:], ident[:])
        for u in range(2):
            cols = slice(u * HALF, (u + 1) * HALF)
            y = sb.tile([P, HALF], F32, name="y%d" % u)
            nc.vector.tensor_tensor(y[:], back[u][:], placed[2][:, cols], ALU.add)
            nc.sync.dma_start(out[:, cols], y[:])
